import numpy as np
import ml_dtypes


def mxq(x, axis, fmt="e4m3"):
    dtype, down = {"e4m3": (ml_dtypes.float8_e4m3fn, 7), "e5m2": (ml_dtypes.float8_e5m2, 14)}[fmt]
    v = np.moveaxis(np.asarray(x, np.float32).astype(ml_dtypes.bfloat16).astype(np.float64), axis, -1)
    blocks = v.reshape(v.shape[:-1] + (-1, 32))
    amax = np.abs(blocks).max(-1, keepdims=True)
    byte = np.maximum(np.where(amax > 0, np.frexp(amax)[1] - 1 + 127, 0) - down, 1)
    scale = np.exp2(byte - 127.0)
    codes = (blocks / scale).astype(np.float32).astype(dtype).astype(np.float64)
    return np.moveaxis((codes * scale).reshape(v.shape), -1, axis)


WIDE = False


def mx_kscale(k):
    if not WIDE:
        return np.ones(k)
    levels = np.array([10, -10, 5, -5, 0])
    if k % 512:
        return np.exp2(np.random.permutation(np.resize(levels, k // 32))).repeat(32)
    a = np.empty((k // 512, 16))
    for p in range(k // 512):
        a[p, :8] = np.random.permutation(np.resize(levels, 8))
        for g in range(8):
            far = levels[np.abs(levels - a[p, g]) >= 10]
            a[p, g + 8] = far[np.random.randint(len(far))]
    return np.exp2(a.ravel()).repeat(32)


def f64(x):
    return np.asarray(x).astype(np.float64)


def striped(idx):
    return np.tile(idx.reshape(-1, 16).T, (8, 1)).astype(np.uint16)


def unstriped(offs):
    return offs[:16].T.reshape(-1).astype(np.int64)


def striped8(idx):
    return np.concatenate([x.reshape(-1, 16).T for x in idx]).astype(np.uint16)


def runs(offs, k):
    lists = np.stack([offs[16 * r : 16 * r + 16].T.reshape(-1) for r in range(8)]).astype(np.int64)
    return lists[np.arange(k) % 512 // 64]


def pack_weight(w):
    k, n = w.shape
    w = f64(np.asarray(w, np.float32).astype(ml_dtypes.bfloat16)).reshape(k // 32, 32, n)
    amax = np.abs(w).max(1)
    byte = np.clip(np.where(amax > 0, np.frexp(amax)[1] - 1 + 127 - 7, 1), 1, 254)
    scaled = (w * np.exp2(127.0 - byte)[:, None, :]).reshape(k, n).astype(np.float32)
    words = np.ascontiguousarray(scaled.reshape(k // 512, 128, 4, n).transpose(0, 1, 3, 2)).astype(ml_dtypes.float8_e4m3fn).view(np.uint8)
    return words, np.ascontiguousarray(byte.astype(np.uint8).reshape(k // 512, 16, n))


def unpack_weight(words, scales):
    g, p, n, _ = words.shape
    vals = np.ascontiguousarray(words).view(ml_dtypes.float8_e4m3fn).astype(np.float64) * np.repeat(np.exp2(scales.astype(np.float64) - 127.0), 8, axis=1)[..., None]
    return vals.transpose(0, 1, 3, 2).reshape(g * 512, n)


def relu(v):
    return np.maximum(v, 0.0)


def sigmoid(v):
    return 1.0 / (1.0 + np.exp(-np.maximum(v, -700.0)))


K, T, S, N, H = 512, 2048, 512, 512, 512


def setup_inputs():
    n = np.random.standard_normal
    s = mx_kscale(K)[:, None]
    u = mx_kscale(H)
    packed_xT = pack_weight(n((K, T)) * s)
    return {
        "x_words": packed_xT[0],
        "x_scales": packed_xT[1],
        "w1": (n((K, H)) / np.sqrt(K) / s).astype(np.float32),
        "gn": (np.random.uniform(0.5, 1.5, (H, 1)) * u[:, None]).astype(np.float32),
        "w2": (n((H, N)) / np.sqrt(H) / u[:, None]).astype(np.float32),
        "offs": striped(np.random.permutation(T)[:S]),
        "pos": striped8(np.stack([np.random.permutation(S) for _ in range(8)])),
        "neg": striped8(np.stack([np.random.permutation(S) for _ in range(8)])),
    }


def reference(x_words, x_scales, w1, gn, w2, offs, pos, neg):
    xq = unpack_weight(x_words, x_scales)[:, unstriped(offs)]
    y = mxq(f64(w1), 0, "e4m3").T @ xq
    dp = np.abs(y - (y[np.arange(H)[:, None], runs(pos, H)]))
    dn = np.abs(y - (y[np.arange(H)[:, None], runs(neg, H)]))
    z = f64(gn) * (relu(dp - dn + 0.5) * sigmoid(dp))
    return mxq(f64(w2), 0, "e4m3").T @ mxq(z, 0, "e4m3")

@@ -1,0 +1,190 @@
+from contextlib import ExitStack
+
+import concourse.mybir as mybir
+
+K, T, S, N, H = 512, 2048, 512, 512, 512
+FLOPS = 2 * K * H * S + 2 * H * N * S
+
+F32 = mybir.dt.float32
+BF16 = mybir.dt.bfloat16
+I32 = mybir.dt.int32
+U32 = mybir.dt.uint32
+U16 = mybir.dt.uint16
+U8 = mybir.dt.uint8
+FP8X4 = mybir.dt.float8_e4m3fn_x4
+ALU = mybir.AluOpType
+ACT = mybir.ActivationFunctionType
+
+P = 128
+PACK = 4
+HALF = S // 2
+CHUNKS = (128, 128, 128, 128)
+
+
+def tile_picked_triplet8_none_p_kernel(tc, x_words, x_scales, w1, gn, w2, offs, pos, neg, out):
+    nc = tc.nc
+    with ExitStack() as ctx:
+        keep = ctx.enter_context(tc.tile_pool(name="keep", bufs=1))
+        psum = ctx.enter_context(tc.psum_pool(name="psum", bufs=1))
+
+        offs_sb = keep.tile([P, S // 16], U16, name="offs_sb")
+        pos_sb = keep.tile([P, S // 16], U16, name="pos_sb")
+        neg_sb = keep.tile([P, S // 16], U16, name="neg_sb")
+        words_all = keep.tile([P, T], U32, name="words_all", align_bytes=64)
+        scales_all = keep.tile([P, T], U8, name="scales_all", align_bytes=64)
+        w1_raw = [keep.tile([P, PACK, H // 2], F32, name="w1_raw%d" % h, align_bytes=64) for h in range(2)]
+        w2_raw = keep.tile([P, PACK, N], F32, name="w2_raw", align_bytes=64)
+        gain = keep.tile([P, PACK], F32, name="gain")
+        zero = keep.tile([P, 1], F32, name="zero")
+        margin = keep.tile([P, 1], F32, name="margin")
+
+        nc.vector.memset(scales_all[:].bitcast(I32), 0)
+        nc.vector.memset(zero[:], 0.0)
+        nc.sync.dma_start(offs_sb[:], offs)
+        nc.sync.dma_start(words_all[:].bitcast(I32), x_words[0].rearrange("p n r -> p (n r)").bitcast(I32))
+        for q in range(4):
+            nc.scalar.dma_start(scales_all[32 * q : 32 * q + 4, :].bitcast(I32), x_scales[0, 4 * q : 4 * q + 4, :].bitcast(I32))
+        nc.scalar.activation(margin[:], zero[:], ACT.Sigmoid)
+        w1_rows = w1.rearrange("(p j) c -> p j c", j=PACK)
+        for h in range(2):
+            nc.sync.dma_start(w1_raw[h][:], w1_rows[:, :, h * (H // 2) : (h + 1) * (H // 2)])
+        nc.sync.dma_start(pos_sb[:], pos)
+        nc.sync.dma_start(neg_sb[:], neg)
+        nc.sync.dma_start(gain[:], gn.rearrange("(p t) o -> p (t o)", t=PACK))
+        nc.sync.dma_start(w2_raw[:], w2.rearrange("(p j) c -> p j c", j=PACK))
+
+        x_codes = keep.tile([P, S], U32, name="x_codes", align_bytes=64)
+        x_bytes = keep.tile([P, S], U8, name="x_bytes", align_bytes=64)
+        nc.vector.tensor_copy(x_bytes[:], scales_all[:].indirect(offs_sb[:]))
+        nc.vector.tensor_copy(x_codes[:], words_all[:].indirect(offs_sb[:]))
+
+        w1_bf = [keep.tile([P, 2, P, PACK], BF16, name="w1_bf%d" % u, align_bytes=64) for u in range(2)]
+
+        def deal_w1(engine_copy, u, h):
+            src = w1_raw[h][:].rearrange("p j (m t) -> p m j t", t=PACK)[:, :, :, 2 * u : 2 * u + 2]
+            dst = w1_bf[u][:, :, 64 * h : 64 * (h + 1), :].rearrange("p e m j -> p m j e")
+            engine_copy(dst, src)
+
+        deal_w1(nc.scalar.copy, 0, 0)
+        deal_w1(nc.scalar.copy, 1, 0)
+        deal_w1(nc.vector.tensor_copy, 0, 1)
+        deal_w1(nc.scalar.copy, 1, 1)
+
+        w1_codes = [keep.tile([P, P], U32, name="w1_codes%d" % t, align_bytes=64) for t in range(PACK)]
+        w1_bytes = [keep.tile([P, P], U8, name="w1_bytes%d" % t, align_bytes=64) for t in range(PACK)]
+
+        def quantise_w1(t):
+            nc.vector.quantize_mx(
+                out=w1_codes[t][:].bitcast(FP8X4),
+                scales=w1_bytes[t][:],
+                in_=w1_bf[t // 2][:, t % 2, :, :].rearrange("p m j -> p (m j)"),
+            )
+
+        def project(t, cols, bank):
+            nc.tensor.matmul_mx(
+                out=bank,
+                lhsT=w1_codes[t][:].bitcast(FP8X4),
+                lhsT_scale=w1_bytes[t][:],
+                rhs=x_codes[:, cols].bitcast(FP8X4),
+                rhs_scale=x_bytes[:, cols],
+                start=True,
+                stop=True,
+            )
+
+        windows = [keep.tile([P, S if t == 0 else 2 * S], F32, name="window%d" % t, align_bytes=64) for t in range(PACK)]
+        last_twin = keep.tile([P, S], F32, name="last_twin", align_bytes=64)
+        twins = [windows[t + 1][:, S : 2 * S] for t in range(PACK - 1)] + [last_twin[:]]
+        lo, hi = slice(0, HALF), slice(HALF, S)
+
+        quantise_w1(0)
+        bank_lo = psum.tile([P, HALF], F32, name="bank_lo", tag="b0")
+        bank_hi = psum.tile([P, HALF], F32, name="bank_hi", tag="b1")
+        project(0, lo, bank_lo[:])
+        project(0, hi, bank_hi[:])
+        nc.vector.tensor_copy(windows[0][:, lo], bank_lo[:])
+        nc.scalar.copy(windows[0][:, hi], bank_hi[:])
+        nc.vector.tensor_copy(twins[0][:, lo], windows[0][:, lo])
+        nc.scalar.copy(twins[0][:, hi], bank_hi[:])
+        for t in range(1, PACK):
+            quantise_w1(t)
+            bank = psum.tile([P, S], F32, name="bank_y", tag="b%d" % (t + 1))
+            project(t, slice(0, S), bank[:])
+            nc.scalar.copy(windows[t][:, 0:S], bank[:])
+            nc.scalar.copy(twins[t], bank[:])
+
+        diffs = [keep.tile([P, 2, S], F32, name="diffs%d" % t, align_bytes=64) for t in range(PACK)]
+        for t in range(PACK):
+            pieces = (lo, hi) if t == 0 else (slice(0, S),)
+            for cols in pieces:
+                for side, lists in enumerate((pos_sb, neg_sb)):
+                    nc.vector.tensor_tensor(
+                        diffs[t][:, side, cols],
+                        windows[t][:].indirect(lists[:, cols.start // 16 : cols.stop // 16]),
+                        twins[t][:, cols],
+                        ALU.subtract,
+                    )
+
+        dist = [keep.tile([P, 2, S], F32, name="dist%d" % t, align_bytes=64) for t in range(PACK)]
+        gate = keep.tile([P, PACK, S], F32, name="gate", align_bytes=64)
+        gap = keep.tile([P, PACK, S], F32, name="gap", align_bytes=64)
+        hinge = keep.tile([P, PACK, S], F32, name="hinge", align_bytes=64)
+        w2_bf = keep.tile([P, N, PACK], BF16, name="w2_bf", align_bytes=64)
+        w2_codes = keep.tile([P, N], U32, name="w2_codes", align_bytes=64)
+        w2_bytes = keep.tile([P, N], U8, name="w2_bytes", align_bytes=64)
+        for t in range(PACK):
+            nc.scalar.activation(dist[t][:], diffs[t][:], ACT.Abs)
+            nc.scalar.activation(gate[:, t, :], dist[t][:, 0, :], ACT.Sigmoid)
+            if t < 2:
+                cols = slice(t * N // 2, (t + 1) * N // 2)
+                nc.scalar.copy(
+                    w2_bf[:, cols, :].rearrange("p (c i) j -> p c j i", i=4),
+                    w2_raw[:, :, cols].rearrange("p j (c i) -> p c j i", i=4),
+                )
+        for t in range(PACK):
+            nc.vector.scalar_tensor_tensor(gap[:, t, :], dist[t][:, 0, :], margin[:], dist[t][:, 1, :], ALU.add, ALU.subtract)
+            if t == 1:
+                nc.vector.quantize_mx(out=w2_codes[:].bitcast(FP8X4), scales=w2_bytes[:], in_=w2_bf[:].rearrange("p n j -> p (n j)"))
+            if t > 0:
+                nc.vector.tensor_scalar(hinge[:, t - 1, :], gap[:, t - 1, :], 0.0, gain[:, t - 1 : t], ALU.max, ALU.mult)
+        nc.vector.tensor_scalar(hinge[:, PACK - 1, :], gap[:, PACK - 1, :], 0.0, gain[:, PACK - 1 : PACK], ALU.max, ALU.mult)
+
+        out_rows = out.rearrange("(b p) j -> p b j", p=P)
+        starts = [sum(CHUNKS[:c]) for c in range(len(CHUNKS))]
+        z_bf = [keep.tile([P, w, PACK], BF16, name="z_bf%d" % c, align_bytes=64) for c, w in enumerate(CHUNKS)]
+
+        def weave(c):
+            cols = slice(starts[c], starts[c] + CHUNKS[c])
+            nc.vector.tensor_tensor(
+                z_bf[c][:].rearrange("p (c i) t -> p c t i", i=2),
+                hinge[:, :, cols].rearrange("p t (c i) -> p c t i", i=2),
+                gate[:, :, cols].rearrange("p t (c i) -> p c t i", i=2),
+                ALU.mult,
+            )
+
+        def finish(c):
+            width = CHUNKS[c]
+            cols = slice(starts[c], starts[c] + width)
+            z_codes = keep.tile([P, width], U32, name="z_codes%d" % c, align_bytes=64)
+            z_bytes = keep.tile([P, width], U8, name="z_bytes%d" % c, align_bytes=64)
+            nc.vector.quantize_mx(out=z_codes[:].bitcast(FP8X4), scales=z_bytes[:], in_=z_bf[c][:].rearrange("p n t -> p (n t)"))
+            acc = psum.tile([P, N // P, width], F32, name="acc", tag="b%d" % (c + 2 if c < 3 else 5))
+            for b in range(N // P):
+                rows = slice(b * P, (b + 1) * P)
+                nc.tensor.matmul_mx(
+                    out=acc[:, b, :],
+                    lhsT=w2_codes[:, rows].bitcast(FP8X4),
+                    lhsT_scale=w2_bytes[:, rows],
+                    rhs=z_codes[:].bitcast(FP8X4),
+                    rhs_scale=z_bytes[:],
+                    start=True,
+                    stop=True,
+                )
+            res = keep.tile([P, N // P, width], F32, name="res%d" % c, align_bytes=64)
+            nc.scalar.copy(res[:], acc[:])
+            nc.sync.dma_start(out_rows[:, :, cols], res[:])
+
+        weave(0)
+        for c in range(len(CHUNKS)):
+            if c + 1 < len(CHUNKS):
+                weave(c + 1)
+            finish(c)

@@ -18,7 +18,7 @@ ACT = mybir.ActivationFunctionType
 P = 128
 PACK = 4
 HALF = S // 2
-CHUNKS = (128, 128, 128, 128)
+CHUNKS = (256, 128, 128)
 
 
 def tile_picked_triplet8_none_p_kernel(tc, x_words, x_scales, w1, gn, w2, offs, pos, neg, out):
@@ -40,10 +40,10 @@ def tile_picked_triplet8_none_p_kernel(tc, x_words, x_scales, w1, gn, w2, offs, 
 
         nc.vector.memset(scales_all[:].bitcast(I32), 0)
         nc.vector.memset(zero[:], 0.0)
-        nc.sync.dma_start(offs_sb[:], offs)
         nc.sync.dma_start(words_all[:].bitcast(I32), x_words[0].rearrange("p n r -> p (n r)").bitcast(I32))
+        nc.sync.dma_start(offs_sb[:], offs)
         for q in range(4):
-            nc.scalar.dma_start(scales_all[32 * q : 32 * q + 4, :].bitcast(I32), x_scales[0, 4 * q : 4 * q + 4, :].bitcast(I32))
+            nc.sync.dma_start(scales_all[32 * q : 32 * q + 4, :].bitcast(I32), x_scales[0, 4 * q : 4 * q + 4, :].bitcast(I32))
         nc.scalar.activation(margin[:], zero[:], ACT.Sigmoid)
         w1_rows = w1.rearrange("(p j) c -> p j c", j=PACK)
         for h in range(2):
@@ -55,8 +55,8 @@ def tile_picked_triplet8_none_p_kernel(tc, x_words, x_scales, w1, gn, w2, offs, 
 
         x_codes = keep.tile([P, S], U32, name="x_codes", align_bytes=64)
         x_bytes = keep.tile([P, S], U8, name="x_bytes", align_bytes=64)
-        nc.vector.tensor_copy(x_bytes[:], scales_all[:].indirect(offs_sb[:]))
         nc.vector.tensor_copy(x_codes[:], words_all[:].indirect(offs_sb[:]))
+        nc.vector.tensor_copy(x_bytes[:], scales_all[:].indirect(offs_sb[:]))
 
         w1_bf = [keep.tile([P, 2, P, PACK], BF16, name="w1_bf%d" % u, align_bytes=64) for u in range(2)]
 
@@ -91,8 +91,8 @@ def tile_picked_triplet8_none_p_kernel(tc, x_words, x_scales, w1, gn, w2, offs, 
                 stop=True,
             )
 
-        windows = [keep.tile([P, S if t == 0 else 2 * S], F32, name="window%d" % t, align_bytes=64) for t in range(PACK)]
-        last_twin = keep.tile([P, S], F32, name="last_twin", align_bytes=64)
+        windows = [keep.tile([P, S if t == 0 else 2 * S], F32, name="window%d" % t, tag="window%d" % t, align_bytes=64) for t in range(PACK)]
+        last_twin = keep.tile([P, S], F32, name="last_twin", tag="last_twin", align_bytes=64)
         twins = [windows[t + 1][:, S : 2 * S] for t in range(PACK - 1)] + [last_twin[:]]
         lo, hi = slice(0, HALF), slice(HALF, S)
 
@@ -105,14 +105,19 @@ def tile_picked_triplet8_none_p_kernel(tc, x_words, x_scales, w1, gn, w2, offs, 
         nc.scalar.copy(windows[0][:, hi], bank_hi[:])
         nc.vector.tensor_copy(twins[0][:, lo], windows[0][:, lo])
         nc.scalar.copy(twins[0][:, hi], bank_hi[:])
+        banks = {}
         for t in range(1, PACK):
             quantise_w1(t)
-            bank = psum.tile([P, S], F32, name="bank_y", tag="b%d" % (t + 1))
-            project(t, slice(0, S), bank[:])
-            nc.scalar.copy(windows[t][:, 0:S], bank[:])
-            nc.scalar.copy(twins[t], bank[:])
+            banks[t] = psum.tile([P, S], F32, name="bank_y", tag="b%d" % (t + 1))
+            project(t, slice(0, S), banks[t][:])
+        nc.scalar.copy(windows[1][:, 0:S], banks[1][:])
+        nc.scalar.copy(windows[2][:, 0:S], banks[2][:])
+        nc.sync.dma_start(twins[2], windows[2][:, 0:S])
+        nc.scalar.copy(twins[1], banks[1][:])
+        nc.scalar.copy(windows[3][:, 0:S], banks[3][:])
+        nc.sync.dma_start(twins[3], windows[3][:, 0:S])
 
-        diffs = [keep.tile([P, 2, S], F32, name="diffs%d" % t, align_bytes=64) for t in range(PACK)]
+        diffs = [keep.tile([P, 2, S], F32, name="diffs%d" % t, tag="diffs%d" % t, align_bytes=64) for t in range(PACK)]
         for t in range(PACK):
             pieces = (lo, hi) if t == 0 else (slice(0, S),)
             for cols in pieces:
@@ -124,29 +129,46 @@ def tile_picked_triplet8_none_p_kernel(tc, x_words, x_scales, w1, gn, w2, offs, 
                         ALU.subtract,
                     )
 
-        dist = [keep.tile([P, 2, S], F32, name="dist%d" % t, align_bytes=64) for t in range(PACK)]
+        dist_first = keep.tile([P, PACK - 1, 2, S], F32, name="dist_first", align_bytes=64)
+        dist_last = keep.tile([P, 1, 2, S], F32, name="dist_last", align_bytes=64)
+        dist = [dist_first[:, t, :, :] for t in range(PACK - 1)] + [dist_last[:, 0, :, :]]
         gate = keep.tile([P, PACK, S], F32, name="gate", align_bytes=64)
-        gap = keep.tile([P, PACK, S], F32, name="gap", align_bytes=64)
         hinge = keep.tile([P, PACK, S], F32, name="hinge", align_bytes=64)
-        w2_bf = keep.tile([P, N, PACK], BF16, name="w2_bf", align_bytes=64)
-        w2_codes = keep.tile([P, N], U32, name="w2_codes", align_bytes=64)
         w2_bytes = keep.tile([P, N], U8, name="w2_bytes", align_bytes=64)
+        w2_bf = []
+
+        def round_w2(h, after):
+            cols = slice(h * N // 2, (h + 1) * N // 2)
+            w2_bf.append(keep.tile([P, N // 2, PACK], BF16, name="w2_bf%d" % h, tag="diffs%d" % after, align_bytes=64))
+            nc.scalar.copy(
+                w2_bf[h][:].rearrange("p (c i) j -> p c j i", i=4),
+                w2_raw[:, :, cols].rearrange("p j (c i) -> p c j i", i=4),
+            )
+
         for t in range(PACK):
-            nc.scalar.activation(dist[t][:], diffs[t][:], ACT.Abs)
+            nc.scalar.activation(dist[t], diffs[t][:], ACT.Abs)
             nc.scalar.activation(gate[:, t, :], dist[t][:, 0, :], ACT.Sigmoid)
-            if t < 2:
-                cols = slice(t * N // 2, (t + 1) * N // 2)
-                nc.scalar.copy(
-                    w2_bf[:, cols, :].rearrange("p (c i) j -> p c j i", i=4),
-                    w2_raw[:, :, cols].rearrange("p j (c i) -> p c j i", i=4),
-                )
-        for t in range(PACK):
-            nc.vector.scalar_tensor_tensor(gap[:, t, :], dist[t][:, 0, :], margin[:], dist[t][:, 1, :], ALU.add, ALU.subtract)
             if t == 1:
-                nc.vector.quantize_mx(out=w2_codes[:].bitcast(FP8X4), scales=w2_bytes[:], in_=w2_bf[:].rearrange("p n j -> p (n j)"))
-            if t > 0:
-                nc.vector.tensor_scalar(hinge[:, t - 1, :], gap[:, t - 1, :], 0.0, gain[:, t - 1 : t], ALU.max, ALU.mult)
-        nc.vector.tensor_scalar(hinge[:, PACK - 1, :], gap[:, PACK - 1, :], 0.0, gain[:, PACK - 1 : PACK], ALU.max, ALU.mult)
+                round_w2(0, 1)
+
+        gap_first = keep.tile([P, PACK - 1, S], F32, name="gap_first", tag="window3", align_bytes=64)
+        gap_last = keep.tile([P, 1, S], F32, name="gap_last", align_bytes=64)
+        gaps = [gap_first[:, t, :] for t in range(PACK - 1)] + [gap_last[:, 0, :]]
+        w2_codes = keep.tile([P, N], U32, name="w2_codes", tag="last_twin", align_bytes=64)
+
+        def subtract(gap, both):
+            nc.vector.scalar_tensor_tensor(gap[:], both[:, :, 0, :], margin[:], both[:, :, 1, :], ALU.add, ALU.subtract)
+
+        def quantise_w2(h):
+            cols = slice(h * N // 2, (h + 1) * N // 2)
+            nc.vector.quantize_mx(out=w2_codes[:, cols].bitcast(FP8X4), scales=w2_bytes[:, cols], in_=w2_bf[h][:].rearrange("p n j -> p (n j)"))
+
+        subtract(gap_first, dist_first)
+        round_w2(1, 3)
+        subtract(gap_last, dist_last)
+        for t in range(PACK):
+            nc.vector.tensor_scalar(hinge[:, t, :], gaps[t], 0.0, gain[:, t : t + 1], ALU.max, ALU.mult)
+        quantise_w2(0)
 
         out_rows = out.rearrange("(b p) j -> p b j", p=P)
         starts = [sum(CHUNKS[:c]) for c in range(len(CHUNKS))]
@@ -167,23 +189,35 @@ def tile_picked_triplet8_none_p_kernel(tc, x_words, x_scales, w1, gn, w2, offs, 
             z_codes = keep.tile([P, width], U32, name="z_codes%d" % c, align_bytes=64)
             z_bytes = keep.tile([P, width], U8, name="z_bytes%d" % c, align_bytes=64)
             nc.vector.quantize_mx(out=z_codes[:].bitcast(FP8X4), scales=z_bytes[:], in_=z_bf[c][:].rearrange("p n t -> p (n t)"))
-            acc = psum.tile([P, N // P, width], F32, name="acc", tag="b%d" % (c + 2 if c < 3 else 5))
-            for b in range(N // P):
-                rows = slice(b * P, (b + 1) * P)
-                nc.tensor.matmul_mx(
-                    out=acc[:, b, :],
-                    lhsT=w2_codes[:, rows].bitcast(FP8X4),
-                    lhsT_scale=w2_bytes[:, rows],
-                    rhs=z_codes[:].bitcast(FP8X4),
-                    rhs_scale=z_bytes[:],
-                    start=True,
-                    stop=True,
-                )
-            res = keep.tile([P, N // P, width], F32, name="res%d" % c, align_bytes=64)
-            nc.scalar.copy(res[:], acc[:])
-            nc.sync.dma_start(out_rows[:, :, cols], res[:])
+            last = c == len(CHUNKS) - 1
+            per_bank = 2 if (width == 256 or last) else 4
+            for g in range(N // P // per_bank):
+                acc = psum.tile([P, per_bank, width], F32, name="acc", tag="acc", bufs=3)
+                for b in range(per_bank):
+                    rows = slice((g * per_bank + b) * P, (g * per_bank + b + 1) * P)
+                    nc.tensor.matmul_mx(
+                        out=acc[:, b, :],
+                        lhsT=w2_codes[:, rows].bitcast(FP8X4),
+                        lhsT_scale=w2_bytes[:, rows],
+                        rhs=z_codes[:].bitcast(FP8X4),
+                        rhs_scale=z_bytes[:],
+                        start=True,
+                        stop=True,
+                    )
+                res = keep.tile([P, per_bank, width], F32, name="res%d_%d" % (c, g), align_bytes=64)
+                blocks = slice(g * per_bank, (g + 1) * per_bank)
+                if last and g == 1:
+                    nc.vector.tensor_copy(res[:], acc[:])
+                    nc.sync.dma_start(out_rows[:, blocks, cols], res[:])
+                elif last:
+                    nc.scalar.copy(res[:], acc[:])
+                    nc.scalar.dma_start(out_rows[:, blocks, cols], res[:])
+                else:
+                    nc.scalar.copy(res[:], acc[:])
+                    nc.sync.dma_start(out_rows[:, blocks, cols], res[:])
 
         weave(0)
+        quantise_w2(1)
         for c in range(len(CHUNKS)):
             if c + 1 < len(CHUNKS):
                 weave(c + 1)

@@ -18,7 +18,7 @@ ACT = mybir.ActivationFunctionType
 P = 128
 PACK = 4
 HALF = S // 2
-CHUNKS = (256, 128, 128)
+CHUNKS = (128, 128, 128, 128)
 
 
 def tile_picked_triplet8_none_p_kernel(tc, x_words, x_scales, w1, gn, w2, offs, pos, neg, out):

from contextlib import ExitStack

import concourse.mybir as mybir

K, T, S, N, H = 512, 2048, 512, 512, 512
FLOPS = 2 * K * H * S + 2 * H * N * S

F32 = mybir.dt.float32
BF16 = mybir.dt.bfloat16
I32 = mybir.dt.int32
U32 = mybir.dt.uint32
U16 = mybir.dt.uint16
U8 = mybir.dt.uint8
FP8X4 = mybir.dt.float8_e4m3fn_x4
ALU = mybir.AluOpType
ACT = mybir.ActivationFunctionType

P = 128
PACK = 4
HALF = S // 2
CHUNKS = (128, 128, 128, 128)


def tile_picked_triplet8_none_p_kernel(tc, x_words, x_scales, w1, gn, w2, offs, pos, neg, out):
    nc = tc.nc
    with ExitStack() as ctx:
        keep = ctx.enter_context(tc.tile_pool(name="keep", bufs=1))
        psum = ctx.enter_context(tc.psum_pool(name="psum", bufs=1))

        offs_sb = keep.tile([P, S // 16], U16, name="offs_sb")
        pos_sb = keep.tile([P, S // 16], U16, name="pos_sb")
        neg_sb = keep.tile([P, S // 16], U16, name="neg_sb")
        words_all = keep.tile([P, T], U32, name="words_all", align_bytes=64)
        scales_all = keep.tile([P, T], U8, name="scales_all", align_bytes=64)
        w1_raw = [keep.tile([P, PACK, H // 2], F32, name="w1_raw%d" % h, align_bytes=64) for h in range(2)]
        w2_raw = keep.tile([P, PACK, N], F32, name="w2_raw", align_bytes=64)
        gain = keep.tile([P, PACK], F32, name="gain")
        zero = keep.tile([P, 1], F32, name="zero")
        margin = keep.tile([P, 1], F32, name="margin")

        nc.vector.memset(scales_all[:].bitcast(I32), 0)
        nc.vector.memset(zero[:], 0.0)
        nc.sync.dma_start(words_all[:].bitcast(I32), x_words[0].rearrange("p n r -> p (n r)").bitcast(I32))
        nc.sync.dma_start(offs_sb[:], offs)
        for q in range(4):
            nc.sync.dma_start(scales_all[32 * q : 32 * q + 4, :].bitcast(I32), x_scales[0, 4 * q : 4 * q + 4, :].bitcast(I32))
        nc.scalar.activation(margin[:], zero[:], ACT.Sigmoid)
        w1_rows = w1.rearrange("(p j) c -> p j c", j=PACK)
        for h in range(2):
            nc.sync.dma_start(w1_raw[h][:], w1_rows[:, :, h * (H // 2) : (h + 1) * (H // 2)])
        nc.sync.dma_start(pos_sb[:], pos)
        nc.sync.dma_start(neg_sb[:], neg)
        nc.sync.dma_start(gain[:], gn.rearrange("(p t) o -> p (t o)", t=PACK))
        nc.sync.dma_start(w2_raw[:], w2.rearrange("(p j) c -> p j c", j=PACK))

        x_codes = keep.tile([P, S], U32, name="x_codes", align_bytes=64)
        x_bytes = keep.tile([P, S], U8, name="x_bytes", align_bytes=64)
        nc.vector.tensor_copy(x_codes[:], words_all[:].indirect(offs_sb[:]))
        nc.vector.tensor_copy(x_bytes[:], scales_all[:].indirect(offs_sb[:]))

        w1_bf = [keep.tile([P, 2, P, PACK], BF16, name="w1_bf%d" % u, align_bytes=64) for u in range(2)]

        def deal_w1(engine_copy, u, h):
            src = w1_raw[h][:].rearrange("p j (m t) -> p m j t", t=PACK)[:, :, :, 2 * u : 2 * u + 2]
            dst = w1_bf[u][:, :, 64 * h : 64 * (h + 1), :].rearrange("p e m j -> p m j e")
            engine_copy(dst, src)

        deal_w1(nc.scalar.copy, 0, 0)
        deal_w1(nc.scalar.copy, 1, 0)
        deal_w1(nc.vector.tensor_copy, 0, 1)
        deal_w1(nc.scalar.copy, 1, 1)

        w1_codes = [keep.tile([P, P], U32, name="w1_codes%d" % t, align_bytes=64) for t in range(PACK)]
        w1_bytes = [keep.tile([P, P], U8, name="w1_bytes%d" % t, align_bytes=64) for t in range(PACK)]

        def quantise_w1(t):
            nc.vector.quantize_mx(
                out=w1_codes[t][:].bitcast(FP8X4),
                scales=w1_bytes[t][:],
                in_=w1_bf[t // 2][:, t % 2, :, :].rearrange("p m j -> p (m j)"),
            )

        def project(t, cols, bank):
            nc.tensor.matmul_mx(
                out=bank,
                lhsT=w1_codes[t][:].bitcast(FP8X4),
                lhsT_scale=w1_bytes[t][:],
                rhs=x_codes[:, cols].bitcast(FP8X4),
                rhs_scale=x_bytes[:, cols],
                start=True,
                stop=True,
            )

        windows = [keep.tile([P, S if t == 0 else 2 * S], F32, name="window%d" % t, tag="window%d" % t, align_bytes=64) for t in range(PACK)]
        last_twin = keep.tile([P, S], F32, name="last_twin", tag="last_twin", align_bytes=64)
        twins = [windows[t + 1][:, S : 2 * S] for t in range(PACK - 1)] + [last_twin[:]]
        lo, hi = slice(0, HALF), slice(HALF, S)

        quantise_w1(0)
        bank_lo = psum.tile([P, HALF], F32, name="bank_lo", tag="b0")
        bank_hi = psum.tile([P, HALF], F32, name="bank_hi", tag="b1")
        project(0, lo, bank_lo[:])
        project(0, hi, bank_hi[:])
        nc.vector.tensor_copy(windows[0][:, lo], bank_lo[:])
        nc.scalar.copy(windows[0][:, hi], bank_hi[:])
        nc.vector.tensor_copy(twins[0][:, lo], windows[0][:, lo])
        nc.scalar.copy(twins[0][:, hi], bank_hi[:])
        banks = {}
        for t in range(1, PACK):
            quantise_w1(t)
            banks[t] = psum.tile([P, S], F32, name="bank_y", tag="b%d" % (t + 1))
            project(t, slice(0, S), banks[t][:])
        nc.scalar.copy(windows[1][:, 0:S], banks[1][:])
        nc.scalar.copy(windows[2][:, 0:S], banks[2][:])
        nc.sync.dma_start(twins[2], windows[2][:, 0:S])
        nc.scalar.copy(twins[1], banks[1][:])
        nc.scalar.copy(windows[3][:, 0:S], banks[3][:])
        nc.sync.dma_start(twins[3], windows[3][:, 0:S])

        diffs = [keep.tile([P, 2, S], F32, name="diffs%d" % t, tag="diffs%d" % t, align_bytes=64) for t in range(PACK)]
        for t in range(PACK):
            pieces = (lo, hi) if t == 0 else (slice(0, S),)
            for cols in pieces:
                for side, lists in enumerate((pos_sb, neg_sb)):
                    nc.vector.tensor_tensor(
                        diffs[t][:, side, cols],
                        windows[t][:].indirect(lists[:, cols.start // 16 : cols.stop // 16]),
                        twins[t][:, cols],
                        ALU.subtract,
                    )

        dist_first = keep.tile([P, PACK - 1, 2, S], F32, name="dist_first", align_bytes=64)
        dist_last = keep.tile([P, 1, 2, S], F32, name="dist_last", align_bytes=64)
        dist = [dist_first[:, t, :, :] for t in range(PACK - 1)] + [dist_last[:, 0, :, :]]
        gate = keep.tile([P, PACK, S], F32, name="gate", align_bytes=64)
        hinge = keep.tile([P, PACK, S], F32, name="hinge", align_bytes=64)
        w2_bytes = keep.tile([P, N], U8, name="w2_bytes", align_bytes=64)
        w2_bf = []

        def round_w2(h, after):
            cols = slice(h * N // 2, (h + 1) * N // 2)
            w2_bf.append(keep.tile([P, N // 2, PACK], BF16, name="w2_bf%d" % h, tag="diffs%d" % after, align_bytes=64))
            nc.scalar.copy(
                w2_bf[h][:].rearrange("p (c i) j -> p c j i", i=4),
                w2_raw[:, :, cols].rearrange("p j (c i) -> p c j i", i=4),
            )

        for t in range(PACK):
            nc.scalar.activation(dist[t], diffs[t][:], ACT.Abs)
            nc.scalar.activation(gate[:, t, :], dist[t][:, 0, :], ACT.Sigmoid)
            if t == 1:
                round_w2(0, 1)

        gap_first = keep.tile([P, PACK - 1, S], F32, name="gap_first", tag="window3", align_bytes=64)
        gap_last = keep.tile([P, 1, S], F32, name="gap_last", align_bytes=64)
        gaps = [gap_first[:, t, :] for t in range(PACK - 1)] + [gap_last[:, 0, :]]
        w2_codes = keep.tile([P, N], U32, name="w2_codes", tag="last_twin", align_bytes=64)

        def subtract(gap, both):
            nc.vector.scalar_tensor_tensor(gap[:], both[:, :, 0, :], margin[:], both[:, :, 1, :], ALU.add, ALU.subtract)

        def quantise_w2(h):
            cols = slice(h * N // 2, (h + 1) * N // 2)
            nc.vector.quantize_mx(out=w2_codes[:, cols].bitcast(FP8X4), scales=w2_bytes[:, cols], in_=w2_bf[h][:].rearrange("p n j -> p (n j)"))

        subtract(gap_first, dist_first)
        round_w2(1, 3)
        subtract(gap_last, dist_last)
        for t in range(PACK):
            nc.vector.tensor_scalar(hinge[:, t, :], gaps[t], 0.0, gain[:, t : t + 1], ALU.max, ALU.mult)
        quantise_w2(0)

        out_rows = out.rearrange("(b p) j -> p b j", p=P)
        starts = [sum(CHUNKS[:c]) for c in range(len(CHUNKS))]
        z_bf = [keep.tile([P, w, PACK], BF16, name="z_bf%d" % c, align_bytes=64) for c, w in enumerate(CHUNKS)]

        def weave(c):
            cols = slice(starts[c], starts[c] + CHUNKS[c])
            nc.vector.tensor_tensor(
                z_bf[c][:].rearrange("p (c i) t -> p c t i", i=2),
                hinge[:, :, cols].rearrange("p t (c i) -> p c t i", i=2),
                gate[:, :, cols].rearrange("p t (c i) -> p c t i", i=2),
                ALU.mult,
            )

        def finish(c):
            width = CHUNKS[c]
            cols = slice(starts[c], starts[c] + width)
            z_codes = keep.tile([P, width], U32, name="z_codes%d" % c, align_bytes=64)
            z_bytes = keep.tile([P, width], U8, name="z_bytes%d" % c, align_bytes=64)
            nc.vector.quantize_mx(out=z_codes[:].bitcast(FP8X4), scales=z_bytes[:], in_=z_bf[c][:].rearrange("p n t -> p (n t)"))
            last = c == len(CHUNKS) - 1
            per_bank = 2 if (width == 256 or last) else 4
            for g in range(N // P // per_bank):
                acc = psum.tile([P, per_bank, width], F32, name="acc", tag="acc", bufs=3)
                for b in range(per_bank):
                    rows = slice((g * per_bank + b) * P, (g * per_bank + b + 1) * P)
                    nc.tensor.matmul_mx(
                        out=acc[:, b, :],
                        lhsT=w2_codes[:, rows].bitcast(FP8X4),
                        lhsT_scale=w2_bytes[:, rows],
                        rhs=z_codes[:].bitcast(FP8X4),
                        rhs_scale=z_bytes[:],
                        start=True,
                        stop=True,
                    )
                res = keep.tile([P, per_bank, width], F32, name="res%d_%d" % (c, g), align_bytes=64)
                blocks = slice(g * per_bank, (g + 1) * per_bank)
                if last and g == 1:
                    nc.vector.tensor_copy(res[:], acc[:])
                    nc.sync.dma_start(out_rows[:, blocks, cols], res[:])
                elif last:
                    nc.scalar.copy(res[:], acc[:])
                    nc.scalar.dma_start(out_rows[:, blocks, cols], res[:])
                else:
                    nc.scalar.copy(res[:], acc[:])
                    nc.sync.dma_start(out_rows[:, blocks, cols], res[:])

        weave(0)
        quantise_w2(1)
        for c in range(len(CHUNKS)):
            if c + 1 < len(CHUNKS):
                weave(c + 1)
            finish(c)
